import numpy as np
import ml_dtypes


def mxq(x, axis, fmt="e4m3"):
    dtype, down = {"e4m3": (ml_dtypes.float8_e4m3fn, 7), "e5m2": (ml_dtypes.float8_e5m2, 14)}[fmt]
    v = np.moveaxis(np.asarray(x, np.float32).astype(ml_dtypes.bfloat16).astype(np.float64), axis, -1)
    blocks = v.reshape(v.shape[:-1] + (-1, 32))
    amax = np.abs(blocks).max(-1, keepdims=True)
    byte = np.maximum(np.where(amax > 0, np.frexp(amax)[1] - 1 + 127, 0) - down, 1)
    scale = np.exp2(byte - 127.0)
    codes = (blocks / scale).astype(np.float32).astype(dtype).astype(np.float64)
    return np.moveaxis((codes * scale).reshape(v.shape), -1, axis)


WIDE = False


def mx_kscale(k):
    if not WIDE:
        return np.ones(k)
    levels = np.array([10, -10, 5, -5, 0])
    if k % 512:
        return np.exp2(np.random.permutation(np.resize(levels, k // 32))).repeat(32)
    a = np.empty((k // 512, 16))
    for p in range(k // 512):
        a[p, :8] = np.random.permutation(np.resize(levels, 8))
        for g in range(8):
            far = levels[np.abs(levels - a[p, g]) >= 10]
            a[p, g + 8] = far[np.random.randint(len(far))]
    return np.exp2(a.ravel()).repeat(32)


BF16 = ml_dtypes.bfloat16


def bf(x):
    return np.asarray(x, np.float32).astype(BF16)


def f64(x):
    return np.asarray(x).astype(np.float64)

E4M3FN = np.array([(-1.0 if i & 128 else 1.0) * ((1.0 + (i & 7) / 8.0) * 2.0 ** (((i >> 3) & 15) - 7) if i & 120 else (i & 7) * 2.0 ** -9) for i in range(256)])


def e4m3fn_bytes(y):
    return np.clip(np.asarray(y, np.float64), -448.0, 448.0).astype(np.float32).astype(ml_dtypes.float8_e4m3fn).view(np.uint8)


def e4m3fn_values(b):
    return E4M3FN[b]


T, K, V, G = 512, 2048, 4096, 128

CAP = 8.0


def setup_inputs():
    s = mx_kscale(K)
    x = np.random.standard_normal((T, K)) * s
    x_scale = (np.abs(x).reshape(T, K // G, G).max(axis=2) / 448.0).astype(np.float32)
    x_bytes = e4m3fn_bytes(x / np.repeat(x_scale.astype(np.float64), G, axis=1))
    emb = bf(np.random.standard_normal((V, K)) * (0.5 * CAP) / np.sqrt(K) / s)
    inv_temp = bf(np.exp(0.25 * np.random.standard_normal((T, 1))))
    return {"x_bytes": x_bytes,
            "x_scale": x_scale,
            "emb": emb,
            "inv_temp": inv_temp}


def reference(x_bytes, x_scale, emb, inv_temp):
    x = e4m3fn_values(x_bytes) * np.repeat(f64(x_scale), G, axis=1)
    xq = mxq(x, 1, "e4m3")
    eq = mxq(f64(emb), 1, "e4m3")
    z = xq @ eq.T
    capped = CAP * np.tanh(z / CAP)
    return capped * f64(inv_temp)

@@ -1,0 +1,248 @@
+from contextlib import ExitStack
+
+import concourse.mybir as mybir
+from concourse.masks import make_identity
+
+T, K, V = 512, 2048, 4096
+FLOPS = 2 * T * K * V
+
+F32 = mybir.dt.float32
+BF16 = mybir.dt.bfloat16
+U32 = mybir.dt.uint32
+U8 = mybir.dt.uint8
+FP8 = mybir.dt.float8_e4m3fn
+FP8X4 = mybir.dt.float8_e4m3fn_x4
+ACT = mybir.ActivationFunctionType
+ALU = mybir.AluOpType
+
+P = 128
+G = K // 512
+M = T // P
+N = 512
+NT = V // N
+CAP = 8.0
+T_BANKS = 5
+A_BANKS = 3
+V_COPY_BANKS = (7,)
+
+
+def tile_softcap_lm_head_d1_kernel(tc, x_bytes, x_scale, emb, inv_temp, out):
+    nc = tc.nc
+    with ExitStack() as ctx:
+        const = ctx.enter_context(tc.tile_pool(name="const", bufs=1))
+        xpool = ctx.enter_context(tc.tile_pool(name="xpool", bufs=1))
+        rawp = ctx.enter_context(tc.tile_pool(name="rawp", bufs=10))
+        regp = ctx.enter_context(tc.tile_pool(name="regp", bufs=4))
+        grpp = ctx.enter_context(tc.tile_pool(name="grpp", bufs=8))
+        codep = ctx.enter_context(tc.tile_pool(name="codep", bufs=8))
+        outp = ctx.enter_context(tc.tile_pool(name="outp", bufs=4))
+        ps_t = ctx.enter_context(tc.psum_pool(name="ps_t", bufs=T_BANKS))
+        ps_a = ctx.enter_context(tc.psum_pool(name="ps_a", bufs=A_BANKS))
+        ctx.enter_context(tc.manual_schedule())
+
+        x_view = x_bytes.rearrange("(p m) k -> p m k", m=M)
+        emb_view = emb.rearrange("(i p r) k -> i p r k", p=P, r=4)
+        out_view = out.rearrange("(p m) v -> p m v", m=M)
+
+        xs = const.tile([P, M, K // 128], F32, name="xs")
+        nc.scalar.dma_start(out=xs[:], in_=x_scale.rearrange("(p m) b -> p m b", m=M))
+        x8 = []
+        for m in range(M):
+            t = xpool.tile([P, K], U8, name="x8_%d" % m)
+            nc.sync.dma_start(out=t[:], in_=x_view[:, m, :])
+            x8.append(t)
+        inv_bf = const.tile([P, M], BF16, name="inv_bf")
+        nc.scalar.dma_start(out=inv_bf[:], in_=inv_temp.rearrange("(p m) o -> p (m o)", m=M))
+
+        raw = {}
+
+        def load(i):
+            for rp in range(2):
+                t = rawp.tile([P, 2, K], BF16, name="raw", align_bytes=64)
+                if i == 0:
+                    for q in range(2):
+                        nc.sync.dma_start(out=t[:, q, :], in_=emb_view[i][:, 2 * rp + q, :])
+                else:
+                    nc.sync.dma_start(out=t[:], in_=emb_view[i][:, 2 * rp : 2 * rp + 2, :])
+                raw[i, rp] = t
+
+        for i in range(5):
+            load(i)
+
+        ident = const.tile([P, P], F32, name="ident")
+        make_identity(nc, ident[:])
+        warm = const.tile([P, 1], F32, name="warm")
+        nc.vector.memset(warm[:], 0.0)
+        warm_out = const.tile([P, 1], F32, name="warm_out")
+        nc.scalar.activation(out=warm_out[:], in_=warm[:], func=ACT.Tanh)
+        inv8 = const.tile([P, M], F32, name="inv8")
+
+        reg = {}
+        grp = {}
+        codes = {}
+        scales = {}
+        bank = {}
+        xw = {}
+
+        def widen(mp, g, n_scalar):
+            t = xpool.tile([P, 2, 512], BF16, name="xw_%d_%d" % (mp, g), align_bytes=64)
+            xw[mp, g] = t
+            n = 0
+            for q in range(2):
+                m = 2 * mp + q
+                for b in range(4):
+                    o = t[:, q, 128 * b : 128 * (b + 1)]
+                    c = 512 * g + 128 * b
+                    src = x8[m][:, c : c + 128].bitcast(FP8)
+                    s = xs[:, m, 4 * g + b : 4 * g + b + 1]
+                    if n < 8 - n_scalar:
+                        nc.vector.tensor_scalar(out=o, in0=src, scalar1=s, scalar2=None, op0=ALU.mult)
+                    else:
+                        nc.scalar.activation(out=o, in_=src, func=ACT.Copy, scale=s)
+                    n += 1
+
+        def reorder(i, r):
+            rp, q = divmod(r, 2)
+            if q == 0:
+                t = regp.tile([P, 2, G, 2, P], F32, name="reg", align_bytes=64)
+                reg[i, rp] = t
+            nc.vector.tensor_copy(
+                out=reg[i, rp][:, q],
+                in_=raw[i, rp][:, q, :].bitcast(F32).rearrange("p (g w u) -> p g u w", g=G, u=2),
+            )
+
+        def words(i, g, rp, q, u):
+            if i == "x":
+                return xw[rp, g][:, q, :].bitcast(F32)[:, u::2]
+            if i == 0:
+                return raw[i, rp][:, q, :].bitcast(F32)[:, 256 * g + u : 256 * (g + 1) : 2]
+            return reg[i, rp][:, q, g, u, :]
+
+        def turn(i, g, rp):
+            t = ps_t.tile([P, 2, 256], F32, name="tbank")
+            bank[i, g, rp] = t
+            for q in range(2):
+                for u in range(2):
+                    nc.tensor.transpose(t[:, u, 128 * q : 128 * (q + 1)], words(i, g, rp, q, u), ident[:])
+
+        def empty(eng, i, g, rp):
+            if (i, g) not in grp:
+                t = grpp.tile([P, 4 * N], BF16, name="grp", align_bytes=64)
+                grp[i, g] = t
+            o = grp[i, g][:].bitcast(F32)[:, 512 * rp : 512 * (rp + 1)].rearrange("p (n u) -> p n u", u=2)
+            src = bank[i, g, rp][:].rearrange("p u n -> p n u")
+            if eng == "S":
+                nc.scalar.copy(out=o, in_=src)
+            else:
+                nc.vector.tensor_copy(out=o, in_=src)
+
+        def quantize(i, g):
+            if i == "x":
+                c = xpool.tile([P, N], U32, name="xc_%d" % g, align_bytes=64)
+                s = xpool.tile([P, N], U8, name="xsc_%d" % g, align_bytes=64)
+            else:
+                c = codep.tile([P, N], U32, name="codes", align_bytes=64)
+                s = codep.tile([P, N], U8, name="scales", align_bytes=64)
+            nc.vector.quantize_mx(out=c[:].bitcast(FP8X4), scales=s[:], in_=grp[i, g][:])
+            codes[i, g] = c
+            scales[i, g] = s
+
+        acc = {}
+        th = {}
+        res = {}
+
+        def multiply(i, m):
+            t = ps_a.tile([P, N], F32, name="acc")
+            acc[i, m] = t
+            for g in range(G):
+                nc.tensor.matmul_mx(
+                    out=t[:],
+                    lhsT=codes["x", g][:, P * m : P * (m + 1)].bitcast(FP8X4),
+                    lhsT_scale=scales["x", g][:, P * m : P * (m + 1)],
+                    rhs=codes[i, g][:].bitcast(FP8X4),
+                    rhs_scale=scales[i, g][:],
+                    start=(g == 0),
+                    stop=(g == G - 1),
+                )
+            h = outp.tile([P, N], F32, name="th")
+            th[i, m] = h
+            nc.scalar.activation(
+                out=h[:].rearrange("p (j r) -> p j r", r=4),
+                in_=t[:].rearrange("p (r j) -> p j r", r=4),
+                func=ACT.Tanh,
+                scale=1.0 / CAP,
+            )
+
+        def finish(i, m):
+            mp, q = divmod(m, 2)
+            if q == 0:
+                t = outp.tile([P, 2, N], F32, name="res")
+                res[i, mp] = t
+            nc.vector.tensor_scalar(
+                out=res[i, mp][:, q, :], in0=th[i, m][:], scalar1=inv8[:, m : m + 1], scalar2=None, op0=ALU.mult
+            )
+            if q == 1:
+                nc.sync.dma_start(out=out_view[:, 2 * mp : 2 * mp + 2, N * i : N * (i + 1)], in_=res[i, mp][:])
+
+        def turn_tile(i, extra):
+            for b in range(8):
+                g, rp = divmod(b, 2)
+                turn(i, g, rp)
+                empty("V" if b in V_COPY_BANKS else "S", i, g, rp)
+                if b % 2 == 1:
+                    if extra:
+                        extra.pop(0)()
+                    if b >= 3:
+                        quantize(i, (b - 3) // 2)
+
+        for g in range(G):
+            widen(0, g, 2)
+            turn("x", g, 0)
+            empty("S", "x", g, 0)
+        for g in range(G):
+            widen(1, g, 1)
+            turn("x", g, 1)
+            empty("S", "x", g, 1)
+            turn(0, g, 0)
+            empty("S", 0, g, 0)
+        nc.vector.tensor_scalar(out=inv8[:], in0=inv_bf[:], scalar1=CAP, scalar2=None, op0=ALU.mult)
+        for g in range(G):
+            turn(0, g, 1)
+            empty("V" if g == 3 else "S", 0, g, 1)
+            quantize("x", g)
+            if g in (1, 3):
+                reorder(1, g // 2)
+        for g in range(G):
+            quantize(0, g)
+        reorder(1, 2)
+        reorder(1, 3)
+        multiply(0, 0)
+        multiply(0, 1)
+        load(5)
+        turn_tile(1, [lambda: reorder(2, 0), lambda: reorder(2, 1), lambda: reorder(2, 2), lambda: reorder(2, 3)])
+        multiply(0, 2)
+        quantize(1, 3)
+        finish(0, 0)
+        finish(0, 1)
+        multiply(0, 3)
+        finish(0, 2)
+
+        for i in range(1, NT):
+            finish(i - 1, 3)
+            if i + 5 < NT:
+                load(i + 5)
+            if i + 1 < NT:
+                fill = []
+                if i + 2 < NT:
+                    fill = [lambda r=r: reorder(i + 2, r) for r in range(4)]
+                turn_tile(i + 1, fill)
+            multiply(i, 0)
+            if i + 1 < NT:
+                quantize(i + 1, 3)
+            multiply(i, 1)
+            finish(i, 0)
+            multiply(i, 2)
+            finish(i, 1)
+            multiply(i, 3)
+            finish(i, 2)
+        finish(NT - 1, 3)

@@ -41,16 +41,20 @@ def tile_softcap_lm_head_d1_kernel(tc, x_bytes, x_scale, emb, inv_temp, out):
         ctx.enter_context(tc.manual_schedule())
 
         x_view = x_bytes.rearrange("(p m) k -> p m k", m=M)
-        emb_view = emb.rearrange("(i p r) k -> i p r k", p=P, r=4)
+        emb_view = emb.rearrange("(i r p) k -> i p r k", p=P, r=4)
         out_view = out.rearrange("(p m) v -> p m v", m=M)
 
         xs = const.tile([P, M, K // 128], F32, name="xs")
         nc.scalar.dma_start(out=xs[:], in_=x_scale.rearrange("(p m) b -> p m b", m=M))
         x8 = []
-        for m in range(M):
+
+        def load_x(m):
             t = xpool.tile([P, K], U8, name="x8_%d" % m)
             nc.sync.dma_start(out=t[:], in_=x_view[:, m, :])
             x8.append(t)
+
+        load_x(0)
+        load_x(1)
         inv_bf = const.tile([P, M], BF16, name="inv_bf")
         nc.scalar.dma_start(out=inv_bf[:], in_=inv_temp.rearrange("(p m) o -> p (m o)", m=M))
 
@@ -66,7 +70,10 @@ def tile_softcap_lm_head_d1_kernel(tc, x_bytes, x_scale, emb, inv_temp, out):
                     nc.sync.dma_start(out=t[:], in_=emb_view[i][:, 2 * rp : 2 * rp + 2, :])
                 raw[i, rp] = t
 
-        for i in range(5):
+        load(0)
+        load_x(2)
+        load_x(3)
+        for i in range(1, 5):
             load(i)
 
         ident = const.tile([P, P], F32, name="ident")
@@ -136,11 +143,21 @@ def tile_softcap_lm_head_d1_kernel(tc, x_bytes, x_scale, emb, inv_temp, out):
             else:
                 nc.vector.tensor_copy(out=o, in_=src)
 
+        def quantize_x(g, mp):
+            if mp == 0:
+                c = xpool.tile([P, T], U32, name="xc_%d" % g, align_bytes=64)
+                s = xpool.tile([P, T], U8, name="xsc_%d" % g, align_bytes=64)
+                codes["x", g] = c
+                scales["x", g] = s
+            cols = slice(256 * mp, 256 * (mp + 1))
+            nc.vector.quantize_mx(
+                out=codes["x", g][:, cols].bitcast(FP8X4),
+                scales=scales["x", g][:, cols],
+                in_=grp["x", g][:, 1024 * mp : 1024 * (mp + 1)],
+            )
+
         def quantize(i, g):
-            if i == "x":
-                c = xpool.tile([P, N], U32, name="xc_%d" % g, align_bytes=64)
-                s = xpool.tile([P, N], U8, name="xsc_%d" % g, align_bytes=64)
-            else:
+            if True:
                 c = codep.tile([P, N], U32, name="codes", align_bytes=64)
                 s = codep.tile([P, N], U8, name="scales", align_bytes=64)
             nc.vector.quantize_mx(out=c[:].bitcast(FP8X4), scales=s[:], in_=grp[i, g][:])
@@ -166,12 +183,7 @@ def tile_softcap_lm_head_d1_kernel(tc, x_bytes, x_scale, emb, inv_temp, out):
                 )
             h = outp.tile([P, N], F32, name="th")
             th[i, m] = h
-            nc.scalar.activation(
-                out=h[:].rearrange("p (j r) -> p j r", r=4),
-                in_=t[:].rearrange("p (r j) -> p j r", r=4),
-                func=ACT.Tanh,
-                scale=1.0 / CAP,
-            )
+            nc.scalar.activation(out=h[:], in_=t[:], func=ACT.Tanh, scale=1.0 / CAP)
 
         def finish(i, m):
             mp, q = divmod(m, 2)
@@ -184,8 +196,8 @@ def tile_softcap_lm_head_d1_kernel(tc, x_bytes, x_scale, emb, inv_temp, out):
             if q == 1:
                 nc.sync.dma_start(out=out_view[:, 2 * mp : 2 * mp + 2, N * i : N * (i + 1)], in_=res[i, mp][:])
 
-        def turn_tile(i, extra):
-            for b in range(8):
+        def turn_half(i, half, extra):
+            for b in range(4 * half, 4 * half + 4):
                 g, rp = divmod(b, 2)
                 turn(i, g, rp)
                 empty("V" if b in V_COPY_BANKS else "S", i, g, rp)
@@ -195,54 +207,64 @@ def tile_softcap_lm_head_d1_kernel(tc, x_bytes, x_scale, emb, inv_temp, out):
                     if b >= 3:
                         quantize(i, (b - 3) // 2)
 
+        widen(0, 0, 3)
         for g in range(G):
-            widen(0, g, 2)
+            if g + 1 < G:
+                widen(0, g + 1, 3)
             turn("x", g, 0)
             empty("S", "x", g, 0)
         for g in range(G):
-            widen(1, g, 1)
-            turn("x", g, 1)
-            empty("S", "x", g, 1)
             turn(0, g, 0)
-            empty("S", 0, g, 0)
-        nc.vector.tensor_scalar(out=inv8[:], in0=inv_bf[:], scalar1=CAP, scalar2=None, op0=ALU.mult)
+            empty("V" if g in (0, 2) else "S", 0, g, 0)
+            quantize_x(g, 0)
+        for g in range(G):
+            widen(1, g, 0)
         for g in range(G):
             turn(0, g, 1)
-            empty("V" if g == 3 else "S", 0, g, 1)
-            quantize("x", g)
-            if g in (1, 3):
-                reorder(1, g // 2)
+            empty("S", 0, g, 1)
         for g in range(G):
             quantize(0, g)
-        reorder(1, 2)
-        reorder(1, 3)
         multiply(0, 0)
         multiply(0, 1)
-        load(5)
-        turn_tile(1, [lambda: reorder(2, 0), lambda: reorder(2, 1), lambda: reorder(2, 2), lambda: reorder(2, 3)])
+        for g in range(G):
+            turn("x", g, 1)
+            empty("S", "x", g, 1)
+        reorder(1, 0)
+        reorder(1, 1)
+        quantize_x(0, 1)
+        quantize_x(1, 1)
+        reorder(1, 2)
+        quantize_x(2, 1)
+        quantize_x(3, 1)
+        reorder(1, 3)
+        nc.vector.tensor_scalar(out=inv8[:], in0=inv_bf[:], scalar1=CAP, scalar2=None, op0=ALU.mult)
         multiply(0, 2)
-        quantize(1, 3)
+        load(5)
+        turn_half(1, 0, [lambda: reorder(2, 0), lambda: reorder(2, 1)])
         finish(0, 0)
         finish(0, 1)
         multiply(0, 3)
+        turn_half(1, 1, [lambda: reorder(2, 2), lambda: reorder(2, 3)])
+        quantize(1, 3)
         finish(0, 2)
 
         for i in range(1, NT):
             finish(i - 1, 3)
             if i + 5 < NT:
                 load(i + 5)
-            if i + 1 < NT:
-                fill = []
-                if i + 2 < NT:
-                    fill = [lambda r=r: reorder(i + 2, r) for r in range(4)]
-                turn_tile(i + 1, fill)
-            multiply(i, 0)
-            if i + 1 < NT:
-                quantize(i + 1, 3)
-            multiply(i, 1)
-            finish(i, 0)
-            multiply(i, 2)
-            finish(i, 1)
-            multiply(i, 3)
-            finish(i, 2)
+            for half in range(2):
+                if i + 1 < NT:
+                    fill = []
+                    if i + 2 < NT:
+                        fill = [lambda r=r: reorder(i + 2, r) for r in (2 * half, 2 * half + 1)]
+                    turn_half(i + 1, half, fill)
+                elif half == 1:
+                    pass
+                multiply(i, 2 * half)
+                if half == 1 and i + 1 < NT:
+                    quantize(i + 1, 3)
+                if half == 1:
+                    finish(i, 1)
+                multiply(i, 2 * half + 1)
+                finish(i, 2 * half)
         finish(NT - 1, 3)

@@ -20,10 +20,11 @@ G = K // 512
 M = T // P
 N = 512
 NT = V // N
+Q = G * NT
 CAP = 8.0
-T_BANKS = 5
-A_BANKS = 3
-V_COPY_BANKS = (7,)
+LEAD = 4
+RUNS = ((3, 6), (3, 6), (2, 4))
+STRIDED = 6
 
 
 def tile_softcap_lm_head_d1_kernel(tc, x_bytes, x_scale, emb, inv_temp, out):
@@ -32,12 +33,12 @@ def tile_softcap_lm_head_d1_kernel(tc, x_bytes, x_scale, emb, inv_temp, out):
         const = ctx.enter_context(tc.tile_pool(name="const", bufs=1))
         xpool = ctx.enter_context(tc.tile_pool(name="xpool", bufs=1))
         rawp = ctx.enter_context(tc.tile_pool(name="rawp", bufs=10))
-        regp = ctx.enter_context(tc.tile_pool(name="regp", bufs=4))
+        regp = ctx.enter_context(tc.tile_pool(name="regp", bufs=8))
         grpp = ctx.enter_context(tc.tile_pool(name="grpp", bufs=8))
-        codep = ctx.enter_context(tc.tile_pool(name="codep", bufs=8))
+        codep = ctx.enter_context(tc.tile_pool(name="codep", bufs=10))
         outp = ctx.enter_context(tc.tile_pool(name="outp", bufs=4))
-        ps_t = ctx.enter_context(tc.psum_pool(name="ps_t", bufs=T_BANKS))
-        ps_a = ctx.enter_context(tc.psum_pool(name="ps_a", bufs=A_BANKS))
+        ps_t = ctx.enter_context(tc.psum_pool(name="ps_t", bufs=5))
+        ps_a = ctx.enter_context(tc.psum_pool(name="ps_a", bufs=3))
         ctx.enter_context(tc.manual_schedule())
 
         x_view = x_bytes.rearrange("(p m) k -> p m k", m=M)
@@ -53,24 +54,23 @@ def tile_softcap_lm_head_d1_kernel(tc, x_bytes, x_scale, emb, inv_temp, out):
             nc.sync.dma_start(out=t[:], in_=x_view[:, m, :])
             x8.append(t)
 
+        raw = {}
+
+        def load(i, pairs=(0, 1), whole=True):
+            for rp in pairs:
+                t = rawp.tile([P, 2, K], BF16, name="raw", align_bytes=64)
+                if whole:
+                    nc.sync.dma_start(out=t[:], in_=emb_view[i][:, 2 * rp : 2 * rp + 2, :])
+                else:
+                    for q in range(2):
+                        nc.sync.dma_start(out=t[:, q, :], in_=emb_view[i][:, 2 * rp + q, :])
+                raw[i, rp] = t
+
         load_x(0)
         load_x(1)
         inv_bf = const.tile([P, M], BF16, name="inv_bf")
         nc.scalar.dma_start(out=inv_bf[:], in_=inv_temp.rearrange("(p m) o -> p (m o)", m=M))
-
-        raw = {}
-
-        def load(i):
-            for rp in range(2):
-                t = rawp.tile([P, 2, K], BF16, name="raw", align_bytes=64)
-                if i == 0:
-                    for q in range(2):
-                        nc.sync.dma_start(out=t[:, q, :], in_=emb_view[i][:, 2 * rp + q, :])
-                else:
-                    nc.sync.dma_start(out=t[:], in_=emb_view[i][:, 2 * rp : 2 * rp + 2, :])
-                raw[i, rp] = t
-
-        load(0)
+        load(0, (0, 1), False)
         load_x(2)
         load_x(3)
         for i in range(1, 5):
@@ -108,22 +108,24 @@ def tile_softcap_lm_head_d1_kernel(tc, x_bytes, x_scale, emb, inv_temp, out):
                         nc.scalar.activation(out=o, in_=src, func=ACT.Copy, scale=s)
                     n += 1
 
-        def reorder(i, r):
-            rp, q = divmod(r, 2)
-            if q == 0:
-                t = regp.tile([P, 2, G, 2, P], F32, name="reg", align_bytes=64)
-                reg[i, rp] = t
-            nc.vector.tensor_copy(
-                out=reg[i, rp][:, q],
-                in_=raw[i, rp][:, q, :].bitcast(F32).rearrange("p (g w u) -> p g u w", g=G, u=2),
-            )
+        def regroup(t):
+            i, g = divmod(t, G)
+            if t < STRIDED or t >= Q:
+                return
+            for rp in range(2):
+                r = regp.tile([P, 2, 2, P], F32, name="reg", align_bytes=64)
+                reg[t, rp] = r
+                nc.vector.tensor_copy(
+                    out=r[:],
+                    in_=raw[i, rp][:, :, 512 * g : 512 * (g + 1)].bitcast(F32).rearrange("p q (w u) -> p q u w", u=2),
+                )
 
         def words(i, g, rp, q, u):
             if i == "x":
                 return xw[rp, g][:, q, :].bitcast(F32)[:, u::2]
-            if i == 0:
+            if G * i + g < STRIDED:
                 return raw[i, rp][:, q, :].bitcast(F32)[:, 256 * g + u : 256 * (g + 1) : 2]
-            return reg[i, rp][:, q, g, u, :]
+            return reg[G * i + g, rp][:, q, u, :]
 
         def turn(i, g, rp):
             t = ps_t.tile([P, 2, 256], F32, name="tbank")
@@ -156,115 +158,154 @@ def tile_softcap_lm_head_d1_kernel(tc, x_bytes, x_scale, emb, inv_temp, out):
                 in_=grp["x", g][:, 1024 * mp : 1024 * (mp + 1)],
             )
 
-        def quantize(i, g):
-            if True:
-                c = codep.tile([P, N], U32, name="codes", align_bytes=64)
-                s = codep.tile([P, N], U8, name="scales", align_bytes=64)
+        def quantize(t):
+            if t >= Q:
+                return
+            i, g = divmod(t, G)
+            c = codep.tile([P, N], U32, name="codes", align_bytes=64)
+            s = codep.tile([P, N], U8, name="scales", align_bytes=64)
             nc.vector.quantize_mx(out=c[:].bitcast(FP8X4), scales=s[:], in_=grp[i, g][:])
             codes[i, g] = c
             scales[i, g] = s
 
-        acc = {}
+        def turn_quarter(t, engines=("S", "S")):
+            if t >= Q:
+                return
+            i, g = divmod(t, G)
+            for rp in range(2):
+                turn(i, g, rp)
+                empty(engines[rp], i, g, rp)
+
         th = {}
         res = {}
 
-        def multiply(i, m):
-            t = ps_a.tile([P, N], F32, name="acc")
-            acc[i, m] = t
-            for g in range(G):
-                nc.tensor.matmul_mx(
-                    out=t[:],
-                    lhsT=codes["x", g][:, P * m : P * (m + 1)].bitcast(FP8X4),
-                    lhsT_scale=scales["x", g][:, P * m : P * (m + 1)],
-                    rhs=codes[i, g][:].bitcast(FP8X4),
-                    rhs_scale=scales[i, g][:],
-                    start=(g == 0),
-                    stop=(g == G - 1),
-                )
-            h = outp.tile([P, N], F32, name="th")
-            th[i, m] = h
+        def one_pass(t, n, g, cols):
+            i, m = divmod(n, M)
+            nc.tensor.matmul_mx(
+                out=t[:],
+                lhsT=codes["x", g][:, P * m : P * (m + 1)].bitcast(FP8X4),
+                lhsT_scale=scales["x", g][:, P * m : P * (m + 1)],
+                rhs=codes[i, g][:, cols].bitcast(FP8X4),
+                rhs_scale=scales[i, g][:, cols],
+                start=(g == 0),
+                stop=(g == G - 1),
+            )
+
+        def soften(t, n, cols):
+            h = outp.tile([P, cols.stop - cols.start], F32, name="th")
+            th[n, cols.start] = h
             nc.scalar.activation(out=h[:], in_=t[:], func=ACT.Tanh, scale=1.0 / CAP)
 
-        def finish(i, m):
+        def multiply(n, cols=slice(0, N)):
+            t = ps_a.tile([P, cols.stop - cols.start], F32, name="acc")
+            for g in range(G):
+                one_pass(t, n, g, cols)
+            soften(t, n, cols)
+
+        def finish(n, cols=slice(0, N)):
+            i, m = divmod(n, M)
             mp, q = divmod(m, 2)
             if q == 0:
                 t = outp.tile([P, 2, N], F32, name="res")
                 res[i, mp] = t
             nc.vector.tensor_scalar(
-                out=res[i, mp][:, q, :], in0=th[i, m][:], scalar1=inv8[:, m : m + 1], scalar2=None, op0=ALU.mult
+                out=res[i, mp][:, q, cols], in0=th[n, cols.start][:], scalar1=inv8[:, m : m + 1], scalar2=None, op0=ALU.mult
             )
-            if q == 1:
+            if i == NT - 1:
+                nc.sync.dma_start(out=out_view[:, m, N * i + cols.start : N * i + cols.stop], in_=res[i, mp][:, q, cols])
+            elif q == 1:
                 nc.sync.dma_start(out=out_view[:, 2 * mp : 2 * mp + 2, N * i : N * (i + 1)], in_=res[i, mp][:])
 
-        def turn_half(i, half, extra):
-            for b in range(4 * half, 4 * half + 4):
-                g, rp = divmod(b, 2)
-                turn(i, g, rp)
-                empty("V" if b in V_COPY_BANKS else "S", i, g, rp)
-                if b % 2 == 1:
-                    if extra:
-                        extra.pop(0)()
-                    if b >= 3:
-                        quantize(i, (b - 3) // 2)
 
-        widen(0, 0, 3)
+        widen(0, 0, 1)
         for g in range(G):
             if g + 1 < G:
-                widen(0, g + 1, 3)
+                widen(0, g + 1, 1)
             turn("x", g, 0)
             empty("S", "x", g, 0)
+            if g >= 2:
+                quantize_x(g - 2, 0)
+        quantize_x(2, 0)
         for g in range(G):
             turn(0, g, 0)
             empty("V" if g in (0, 2) else "S", 0, g, 0)
-            quantize_x(g, 0)
+            if g == 0:
+                quantize_x(3, 0)
         for g in range(G):
-            widen(1, g, 0)
-        for g in range(G):
+            widen(1, g, 2)
             turn(0, g, 1)
-            empty("S", 0, g, 1)
-        for g in range(G):
-            quantize(0, g)
-        multiply(0, 0)
-        multiply(0, 1)
+            empty("V" if g in () else "S", 0, g, 1)
         for g in range(G):
             turn("x", g, 1)
-            empty("S", "x", g, 1)
-        reorder(1, 0)
-        reorder(1, 1)
-        quantize_x(0, 1)
-        quantize_x(1, 1)
-        reorder(1, 2)
-        quantize_x(2, 1)
-        quantize_x(3, 1)
-        reorder(1, 3)
+            empty("V" if g in () else "S", "x", g, 1)
+        for g in range(G):
+            quantize(g)
+        for g in range(G):
+            quantize_x(g, 1)
         nc.vector.tensor_scalar(out=inv8[:], in0=inv_bf[:], scalar1=CAP, scalar2=None, op0=ALU.mult)
-        multiply(0, 2)
         load(5)
-        turn_half(1, 0, [lambda: reorder(2, 0), lambda: reorder(2, 1)])
-        finish(0, 0)
-        finish(0, 1)
-        multiply(0, 3)
-        turn_half(1, 1, [lambda: reorder(2, 2), lambda: reorder(2, 3)])
-        quantize(1, 3)
-        finish(0, 2)
+        multiply(0)
+        turn_quarter(4)
+        regroup(6)
+        multiply(1)
+        quantize(4)
+        regroup(7)
+        turn_quarter(5)
+        finish(0)
+        multiply(2)
+        quantize(5)
+        regroup(8)
+        turn_quarter(6)
+        finish(1)
+        multiply(3)
+        quantize(6)
+        regroup(9)
+        turn_quarter(7, ("S", "V"))
 
-        for i in range(1, NT):
-            finish(i - 1, 3)
+        turned = 2 * G * 2
+        emptied = 2 * G * 2 - 2
+        quant = 7
+        grouped = 10
+        done = M * G
+        cur = None
+        fin = 2
+        for i in range(1, NT - 1):
             if i + 5 < NT:
                 load(i + 5)
-            for half in range(2):
-                if i + 1 < NT:
-                    fill = []
-                    if i + 2 < NT:
-                        fill = [lambda r=r: reorder(i + 2, r) for r in (2 * half, 2 * half + 1)]
-                    turn_half(i + 1, half, fill)
-                elif half == 1:
-                    pass
-                multiply(i, 2 * half)
-                if half == 1 and i + 1 < NT:
-                    quantize(i + 1, 3)
-                if half == 1:
-                    finish(i, 1)
-                multiply(i, 2 * half + 1)
-                finish(i, 2 * half)
-        finish(NT - 1, 3)
+            for n_banks, n_passes in RUNS:
+                while 2 * quant + 2 <= turned:
+                    quantize(quant)
+                    quant += 1
+                for b in range(n_banks):
+                    tile, r = divmod(turned, 2 * G)
+                    g, rp = divmod(r, 2)
+                    if tile < NT:
+                        turn(tile, g, rp)
+                        empty("V" if r in (7,) else "S", tile, g, rp)
+                    turned += 1
+                    if b == 0:
+                        while grouped < Q and 2 * grouped < turned + 8:
+                            regroup(grouped)
+                            grouped += 1
+                for p in range(n_passes):
+                    n, g = divmod(done, G)
+                    if g == 0:
+                        cur = ps_a.tile([P, N], F32, name="acc")
+                    one_pass(cur, n, g, slice(0, N))
+                    if g == G - 1:
+                        soften(cur, n, slice(0, N))
+                        finish(fin)
+                        fin += 1
+                    done += 1
+        while quant < Q:
+            quantize(quant)
+            quant += 1
+        for n in range(M * (NT - 1), Q - 1):
+            multiply(n)
+            finish(n - 2)
+        for c in range(0, N, 256):
+            multiply(Q - 1, slice(c, c + 256))
+        finish(Q - 3)
+        finish(Q - 2)
+        for c in range(0, N, 256):
+            finish(Q - 1, slice(c, c + 256))

from contextlib import ExitStack

import concourse.mybir as mybir
from concourse.masks import make_identity

T, K, V = 512, 2048, 4096
FLOPS = 2 * T * K * V

F32 = mybir.dt.float32
BF16 = mybir.dt.bfloat16
U32 = mybir.dt.uint32
U8 = mybir.dt.uint8
FP8 = mybir.dt.float8_e4m3fn
FP8X4 = mybir.dt.float8_e4m3fn_x4
ACT = mybir.ActivationFunctionType
ALU = mybir.AluOpType

P = 128
G = K // 512
M = T // P
N = 512
NT = V // N
Q = G * NT
CAP = 8.0
LEAD = 4
RUNS = ((3, 6), (3, 6), (2, 4))
STRIDED = 6


def tile_softcap_lm_head_d1_kernel(tc, x_bytes, x_scale, emb, inv_temp, out):
    nc = tc.nc
    with ExitStack() as ctx:
        const = ctx.enter_context(tc.tile_pool(name="const", bufs=1))
        xpool = ctx.enter_context(tc.tile_pool(name="xpool", bufs=1))
        rawp = ctx.enter_context(tc.tile_pool(name="rawp", bufs=10))
        regp = ctx.enter_context(tc.tile_pool(name="regp", bufs=8))
        grpp = ctx.enter_context(tc.tile_pool(name="grpp", bufs=8))
        codep = ctx.enter_context(tc.tile_pool(name="codep", bufs=10))
        outp = ctx.enter_context(tc.tile_pool(name="outp", bufs=4))
        ps_t = ctx.enter_context(tc.psum_pool(name="ps_t", bufs=5))
        ps_a = ctx.enter_context(tc.psum_pool(name="ps_a", bufs=3))
        ctx.enter_context(tc.manual_schedule())

        x_view = x_bytes.rearrange("(p m) k -> p m k", m=M)
        emb_view = emb.rearrange("(i r p) k -> i p r k", p=P, r=4)
        out_view = out.rearrange("(p m) v -> p m v", m=M)

        xs = const.tile([P, M, K // 128], F32, name="xs")
        nc.scalar.dma_start(out=xs[:], in_=x_scale.rearrange("(p m) b -> p m b", m=M))
        x8 = []

        def load_x(m):
            t = xpool.tile([P, K], U8, name="x8_%d" % m)
            nc.sync.dma_start(out=t[:], in_=x_view[:, m, :])
            x8.append(t)

        raw = {}

        def load(i, pairs=(0, 1), whole=True):
            for rp in pairs:
                t = rawp.tile([P, 2, K], BF16, name="raw", align_bytes=64)
                if whole:
                    nc.sync.dma_start(out=t[:], in_=emb_view[i][:, 2 * rp : 2 * rp + 2, :])
                else:
                    for q in range(2):
                        nc.sync.dma_start(out=t[:, q, :], in_=emb_view[i][:, 2 * rp + q, :])
                raw[i, rp] = t

        load_x(0)
        load_x(1)
        inv_bf = const.tile([P, M], BF16, name="inv_bf")
        nc.scalar.dma_start(out=inv_bf[:], in_=inv_temp.rearrange("(p m) o -> p (m o)", m=M))
        load(0, (0, 1), False)
        load_x(2)
        load_x(3)
        for i in range(1, 5):
            load(i)

        ident = const.tile([P, P], F32, name="ident")
        make_identity(nc, ident[:])
        warm = const.tile([P, 1], F32, name="warm")
        nc.vector.memset(warm[:], 0.0)
        warm_out = const.tile([P, 1], F32, name="warm_out")
        nc.scalar.activation(out=warm_out[:], in_=warm[:], func=ACT.Tanh)
        inv8 = const.tile([P, M], F32, name="inv8")

        reg = {}
        grp = {}
        codes = {}
        scales = {}
        bank = {}
        xw = {}

        def widen(mp, g, n_scalar):
            t = xpool.tile([P, 2, 512], BF16, name="xw_%d_%d" % (mp, g), align_bytes=64)
            xw[mp, g] = t
            n = 0
            for q in range(2):
                m = 2 * mp + q
                for b in range(4):
                    o = t[:, q, 128 * b : 128 * (b + 1)]
                    c = 512 * g + 128 * b
                    src = x8[m][:, c : c + 128].bitcast(FP8)
                    s = xs[:, m, 4 * g + b : 4 * g + b + 1]
                    if n < 8 - n_scalar:
                        nc.vector.tensor_scalar(out=o, in0=src, scalar1=s, scalar2=None, op0=ALU.mult)
                    else:
                        nc.scalar.activation(out=o, in_=src, func=ACT.Copy, scale=s)
                    n += 1

        def regroup(t):
            i, g = divmod(t, G)
            if t < STRIDED or t >= Q:
                return
            for rp in range(2):
                r = regp.tile([P, 2, 2, P], F32, name="reg", align_bytes=64)
                reg[t, rp] = r
                nc.vector.tensor_copy(
                    out=r[:],
                    in_=raw[i, rp][:, :, 512 * g : 512 * (g + 1)].bitcast(F32).rearrange("p q (w u) -> p q u w", u=2),
                )

        def words(i, g, rp, q, u):
            if i == "x":
                return xw[rp, g][:, q, :].bitcast(F32)[:, u::2]
            if G * i + g < STRIDED:
                return raw[i, rp][:, q, :].bitcast(F32)[:, 256 * g + u : 256 * (g + 1) : 2]
            return reg[G * i + g, rp][:, q, u, :]

        def turn(i, g, rp):
            t = ps_t.tile([P, 2, 256], F32, name="tbank")
            bank[i, g, rp] = t
            for q in range(2):
                for u in range(2):
                    nc.tensor.transpose(t[:, u, 128 * q : 128 * (q + 1)], words(i, g, rp, q, u), ident[:])

        def empty(eng, i, g, rp):
            if (i, g) not in grp:
                t = grpp.tile([P, 4 * N], BF16, name="grp", align_bytes=64)
                grp[i, g] = t
            o = grp[i, g][:].bitcast(F32)[:, 512 * rp : 512 * (rp + 1)].rearrange("p (n u) -> p n u", u=2)
            src = bank[i, g, rp][:].rearrange("p u n -> p n u")
            if eng == "S":
                nc.scalar.copy(out=o, in_=src)
            else:
                nc.vector.tensor_copy(out=o, in_=src)

        def quantize_x(g, mp):
            if mp == 0:
                c = xpool.tile([P, T], U32, name="xc_%d" % g, align_bytes=64)
                s = xpool.tile([P, T], U8, name="xsc_%d" % g, align_bytes=64)
                codes["x", g] = c
                scales["x", g] = s
            cols = slice(256 * mp, 256 * (mp + 1))
            nc.vector.quantize_mx(
                out=codes["x", g][:, cols].bitcast(FP8X4),
                scales=scales["x", g][:, cols],
                in_=grp["x", g][:, 1024 * mp : 1024 * (mp + 1)],
            )

        def quantize(t):
            if t >= Q:
                return
            i, g = divmod(t, G)
            c = codep.tile([P, N], U32, name="codes", align_bytes=64)
            s = codep.tile([P, N], U8, name="scales", align_bytes=64)
            nc.vector.quantize_mx(out=c[:].bitcast(FP8X4), scales=s[:], in_=grp[i, g][:])
            codes[i, g] = c
            scales[i, g] = s

        def turn_quarter(t, engines=("S", "S")):
            if t >= Q:
                return
            i, g = divmod(t, G)
            for rp in range(2):
                turn(i, g, rp)
                empty(engines[rp], i, g, rp)

        th = {}
        res = {}

        def one_pass(t, n, g, cols):
            i, m = divmod(n, M)
            nc.tensor.matmul_mx(
                out=t[:],
                lhsT=codes["x", g][:, P * m : P * (m + 1)].bitcast(FP8X4),
                lhsT_scale=scales["x", g][:, P * m : P * (m + 1)],
                rhs=codes[i, g][:, cols].bitcast(FP8X4),
                rhs_scale=scales[i, g][:, cols],
                start=(g == 0),
                stop=(g == G - 1),
            )

        def soften(t, n, cols):
            h = outp.tile([P, cols.stop - cols.start], F32, name="th")
            th[n, cols.start] = h
            nc.scalar.activation(out=h[:], in_=t[:], func=ACT.Tanh, scale=1.0 / CAP)

        def multiply(n, cols=slice(0, N)):
            t = ps_a.tile([P, cols.stop - cols.start], F32, name="acc")
            for g in range(G):
                one_pass(t, n, g, cols)
            soften(t, n, cols)

        def finish(n, cols=slice(0, N)):
            i, m = divmod(n, M)
            mp, q = divmod(m, 2)
            if q == 0:
                t = outp.tile([P, 2, N], F32, name="res")
                res[i, mp] = t
            nc.vector.tensor_scalar(
                out=res[i, mp][:, q, cols], in0=th[n, cols.start][:], scalar1=inv8[:, m : m + 1], scalar2=None, op0=ALU.mult
            )
            if i == NT - 1:
                nc.sync.dma_start(out=out_view[:, m, N * i + cols.start : N * i + cols.stop], in_=res[i, mp][:, q, cols])
            elif q == 1:
                nc.sync.dma_start(out=out_view[:, 2 * mp : 2 * mp + 2, N * i : N * (i + 1)], in_=res[i, mp][:])


        widen(0, 0, 1)
        for g in range(G):
            if g + 1 < G:
                widen(0, g + 1, 1)
            turn("x", g, 0)
            empty("S", "x", g, 0)
            if g >= 2:
                quantize_x(g - 2, 0)
        quantize_x(2, 0)
        for g in range(G):
            turn(0, g, 0)
            empty("V" if g in (0, 2) else "S", 0, g, 0)
            if g == 0:
                quantize_x(3, 0)
        for g in range(G):
            widen(1, g, 2)
            turn(0, g, 1)
            empty("V" if g in () else "S", 0, g, 1)
        for g in range(G):
            turn("x", g, 1)
            empty("V" if g in () else "S", "x", g, 1)
        for g in range(G):
            quantize(g)
        for g in range(G):
            quantize_x(g, 1)
        nc.vector.tensor_scalar(out=inv8[:], in0=inv_bf[:], scalar1=CAP, scalar2=None, op0=ALU.mult)
        load(5)
        multiply(0)
        turn_quarter(4)
        regroup(6)
        multiply(1)
        quantize(4)
        regroup(7)
        turn_quarter(5)
        finish(0)
        multiply(2)
        quantize(5)
        regroup(8)
        turn_quarter(6)
        finish(1)
        multiply(3)
        quantize(6)
        regroup(9)
        turn_quarter(7, ("S", "V"))

        turned = 2 * G * 2
        emptied = 2 * G * 2 - 2
        quant = 7
        grouped = 10
        done = M * G
        cur = None
        fin = 2
        for i in range(1, NT - 1):
            if i + 5 < NT:
                load(i + 5)
            for n_banks, n_passes in RUNS:
                while 2 * quant + 2 <= turned:
                    quantize(quant)
                    quant += 1
                for b in range(n_banks):
                    tile, r = divmod(turned, 2 * G)
                    g, rp = divmod(r, 2)
                    if tile < NT:
                        turn(tile, g, rp)
                        empty("V" if r in (7,) else "S", tile, g, rp)
                    turned += 1
                    if b == 0:
                        while grouped < Q and 2 * grouped < turned + 8:
                            regroup(grouped)
                            grouped += 1
                for p in range(n_passes):
                    n, g = divmod(done, G)
                    if g == 0:
                        cur = ps_a.tile([P, N], F32, name="acc")
                    one_pass(cur, n, g, slice(0, N))
                    if g == G - 1:
                        soften(cur, n, slice(0, N))
                        finish(fin)
                        fin += 1
                    done += 1
        while quant < Q:
            quantize(quant)
            quant += 1
        for n in range(M * (NT - 1), Q - 1):
            multiply(n)
            finish(n - 2)
        for c in range(0, N, 256):
            multiply(Q - 1, slice(c, c + 256))
        finish(Q - 3)
        finish(Q - 2)
        for c in range(0, N, 256):
            finish(Q - 1, slice(c, c + 256))
